import numpy as np, ml_dtypes
CORES = [2,3,10,11,18,19,26,27,34,35,42,43,50,51,58,59]
N = 16
def setup_inputs(rng):
    return {"x1": rng.standard_normal((N, 128, 16), dtype=np.float32), "x2": rng.standard_normal((N, 128, 16), dtype=np.float32).astype(ml_dtypes.bfloat16)}
def reference(x1, x2):
    out = []
    g = np.concatenate(list(x1), axis=1)
    out.append(np.broadcast_to(g, (N,) + g.shape))
    s = x2.sum(axis=0, dtype=np.float64).astype(x2.dtype)
    b = 16 // N
    out.append(np.stack([s[:, r * b:(r + 1) * b] for r in range(N)]))
    return {"y1": out[0], "y2": out[1]}

@@ -1,0 +1,51 @@
+from concourse.bass import DstId, RemoteDMATransfer
+from concourse.mybir import AluOpType
+
+SCRATCH = {
+    "ag": ("sbuf", [128, 256], "float32"),
+    "x2s": ("sbuf", [128, 16], "bfloat16"),
+    "rs": ("sbuf", [128, 16], "bfloat16"),
+}
+SEMAPHORES = ["ld1", "ld2", "own", "arr1", "arr2", "sent", "acc", "st1", "st2"]
+
+
+def rank_program(g, core, T, topo):
+    r = T.rank_of(core)
+    if r is None:
+        return
+    S = T.sem
+    others = [j for j in range(16) if j != r]
+
+    def did(c):
+        rid, pid, _se = topo.addr(c)
+        return DstId(rid=rid, pnc=pid)
+
+    g.dma_start(T.ag[:, 16 * r:16 * r + 16], T.x1[:]).then_inc(S.ld1, 16)
+    g.dma_start(T.x2s[:], T.x2[:]).then_inc(S.ld2, 16)
+    g.wait_ge(S.ld1, 16)
+    g.remote_dma_fused(
+        [RemoteDMATransfer(dst_ids=[did(T.cores[j]) for j in others], dma_engine_mask=0xFF, remote_sem=S.arr1,
+                           srcs=[T.ag[:, 16 * r:16 * r + 16]],
+                           dsts=[T.ag[:, 16 * r:16 * r + 16] for j in others])],
+        local_sem=S.sent)
+    g.wait_ge(S.ld2, 16)
+    g.dma_start(T.rs[:, r:r + 1], T.x2s[:, r:r + 1]).then_inc(S.own, 16)
+    for part in (others[:8], others[8:]):
+        g.remote_dma_fused(
+            [RemoteDMATransfer(dst_ids=[did(T.cores[j])], dma_engine_mask=1 << k, remote_sem=S.arr2,
+                               src=T.x2s[:, j:j + 1], dst=T.rs[:, r:r + 1])
+             for k, j in enumerate(part)],
+            local_sem=S.sent)
+    g.wait_ge(S.arr1, 15 * 8)
+    g.dma_start(T.y1[:], T.ag[:]).then_inc(S.st1, 16)
+    g.wait_ge(S.own, 16)
+    g.wait_ge(S.arr2, 15)
+    n = 0
+    for w in (8, 4, 2, 1):
+        g.dma_start(T.rs[:, 0:w], T.rs[:, w:2 * w], accum_op=AluOpType.add).then_inc(S.acc, 16)
+        n += 16
+        g.wait_ge(S.acc, n)
+    g.dma_start(T.y2[:], T.rs[:, 0:1]).then_inc(S.st2, 16)
+    g.wait_ge(S.sent, 8 + 15)
+    g.wait_ge(S.st1, 16)
+    g.wait_ge(S.st2, 16)

@@ -1,51 +1,160 @@
 from concourse.bass import DstId, RemoteDMATransfer
-from concourse.mybir import AluOpType
 
 SCRATCH = {
+    "dg": ("dram", [16, 128, 16], "float32"),
     "ag": ("sbuf", [128, 256], "float32"),
     "x2s": ("sbuf", [128, 16], "bfloat16"),
-    "rs": ("sbuf", [128, 16], "bfloat16"),
+    "xab": ("sbuf", [128, 32], "bfloat16"),
+    "part": ("sbuf", [128, 16], "bfloat16"),
+    "y2l": ("sbuf", [128, 2], "bfloat16"),
 }
-SEMAPHORES = ["ld1", "ld2", "own", "arr1", "arr2", "sent", "acc", "st1", "st2"]
+SEMAPHORES = ["ldd", "lda", "ldx", "cp", "st1", "st2",
+              "in1", "in2", "fin",
+              "rx", "rp", "ry",
+              "sent"]
+
+
+def _bits(mask):
+    return bin(mask).count("1")
+
+
+def _plan():
+    prog = {k: [] for k in range(64)}
+
+    def slot(j):
+        return ("dg", j)
+
+    def blk(j, n=1):
+        return ("ag", 16 * j, 16 * (j + n))
+
+    for c in range(8):
+        m = c ^ 1
+
+        def co(k, ch=c):
+            return 8 * (ch % 8) + k
+
+        def both(j):
+            return [(co(2), blk(j)), (co(3), blk(j))]
+
+        a, b = 2 * c, 2 * c + 1
+        far_b = 2 * ((c - 4) % 8) + 1
+        prog[co(2)] += [
+            (["ldd"], [([slot(a)], [(co(4), slot(a)), (co(6, c + 2), slot(a)), (co(7, c + 4), slot(a)),
+                                    (co(5, m), slot(a))], 0x00FF, "in1", 0),
+                       ([slot(a)], [(co(3), blk(a))], 0xFF00, "fin", 0)]),
+            (["ldx"], [([("x2s", 0, 16)], [(co(7), ("xab", 0, 16)), (co(1), ("xab", 0, 16))], 0xFFFF, "rx", 0)]),
+            (["in1"], [([slot(far_b)], [(co(4, m), slot(far_b))], 0x00FF, "in2", 0),
+                       ([slot(far_b)], [(co(3), blk(far_b))], 0xFF00, "fin", 0)]),
+        ]
+        relayed = 2 * ((m - 2) % 8)
+        prog[co(3)] += [
+            (["ldd"], [([slot(b)], [(co(4), slot(b)), (co(6, c + 2), slot(b)), (co(2, c + 4), slot(b)),
+                                    (co(5, m), slot(b))], 0x00FF, "in1", 0),
+                       ([slot(b)], [(co(2), blk(b))], 0xFF00, "fin", 0)]),
+            (["ldx"], [([("x2s", 0, 16)], [(co(7), ("xab", 16, 32)), (co(1), ("xab", 16, 32))], 0xFFFF, "rx", 0)]),
+            (["in2"], [([blk(relayed, 2)], [(co(2), blk(relayed, 2))], 0xFFFF, "fin", 0)]),
+        ]
+        x, y = 2 * ((m - 4) % 8) + 1, 2 * ((m + 2) % 8) + 1
+        prog[co(4)] += [
+            (["in1"], [([slot(a)], [(co(0, c - 2), slot(a))], 0x000F, "in2", 0),
+                       ([slot(b)], [(co(0, c - 2), slot(b))], 0x00F0, "in2", 0)]),
+            (["in2"], [([slot(x)], both(x), 0x00FF, "fin", 0), ([slot(y)], both(y), 0xFF00, "fin", 0)]),
+        ]
+        x, y = 2 * m, 2 * m + 1
+        prog[co(5)] += [
+            (["in1"], [([slot(x)], [(co(0, c - 2), slot(x))], 0x000F, "in2", 0),
+                       ([slot(y)], [(co(4, c - 2), slot(y))], 0x00F0, "in2", 0),
+                       ([slot(x)], both(x), 0x0F00, "fin", 0), ([slot(y)], both(y), 0xF000, "fin", 0)]),
+        ]
+        x, y = 2 * ((c - 2) % 8), 2 * ((c - 2) % 8) + 1
+        prog[co(6)] += [
+            (["in1"], [([slot(x)], [(co(3, m), blk(x))], 0x000F, "in2", 0),
+                       ([slot(y)], [(co(3, m), blk(y))], 0x00F0, "in2", 0),
+                       ([slot(x)], both(x), 0x0F00, "fin", 0), ([slot(y)], both(y), 0xF000, "fin", 0)]),
+        ]
+        x, y = 2 * ((c - 4) % 8), 2 * ((m - 4) % 8)
+        cross = [d for d in range(8) if (d & 1) != (c & 1)]
+        prog[co(7)] += [
+            (["rx"], [([("xab", 2 * d, 2 * d + 2), ("xab", 16 + 2 * d, 16 + 2 * d + 2)],
+                       [(co(1, d), ("part", 2 * c, 2 * c + 2))], 0x3 << (2 * i), "rp", 1)
+                      for i, d in enumerate(cross)]),
+            (["in1"], [([slot(x)], [(co(7, m), slot(x))], 0x00FF, "in2", 0), ([slot(x)], both(x), 0xFF00, "fin", 0)]),
+            (["in2"], [([slot(y)], both(y), 0xFFFF, "fin", 0)]),
+        ]
+        x, y, z = 2 * ((c + 2) % 8), 2 * ((c + 2) % 8) + 1, 2 * ((m + 2) % 8)
+        prog[co(0)] += [
+            (["in2"], [([slot(x)], both(x), 0x000F, "fin", 0), ([slot(y)], both(y), 0x00F0, "fin", 0),
+                       ([slot(z)], both(z), 0x0F00, "fin", 0)]),
+        ]
+        plane = [d for d in range(8) if (d & 1) == (c & 1) and d != c]
+        prog[co(1)] += [
+            (["rx"], [([("xab", 2 * d, 2 * d + 2), ("xab", 16 + 2 * d, 16 + 2 * d + 2)],
+                       [(co(1, d), ("part", 2 * c, 2 * c + 2))], 0x3 << (2 * i), "rp", 1)
+                      for i, d in enumerate(plane)]),
+            (["rp"], [([("part", 2 * d, 2 * d + 2) for d in range(8) if d != c]
+                       + [("xab", 2 * c, 2 * c + 2), ("xab", 16 + 2 * c, 16 + 2 * c + 2)],
+                       [(co(2), ("y2l", 0, 2)), (co(3), ("y2l", 0, 2))], 0xFFFF, "ry", 1)]),
+        ]
+    return prog
+
+
+def _totals(prog):
+    total = {k: {} for k in range(64)}
+    for core, calls in prog.items():
+        for _waits, transfers in calls:
+            for _srcs, dsts, mask, sem, _alu in transfers:
+                total[core]["sent"] = total[core].get("sent", 0) + _bits(mask)
+                for dst, _ap in dsts:
+                    total[dst][sem] = total[dst].get(sem, 0) + _bits(mask)
+    return total
 
 
 def rank_program(g, core, T, topo):
-    r = T.rank_of(core)
-    if r is None:
-        return
+    prog = _plan()
+    total = _totals(prog)[core]
+    for name in ("ldd", "lda", "ldx", "cp", "st1", "st2"):
+        total[name] = 16
     S = T.sem
-    others = [j for j in range(16) if j != r]
+    r = T.rank_of(core)
+
+    def ap(d):
+        if d[0] == "dg":
+            return T.dg[d[1]]
+        return T[d[0]][:, d[1]:d[2]]
 
     def did(c):
         rid, pid, _se = topo.addr(c)
         return DstId(rid=rid, pnc=pid)
 
-    g.dma_start(T.ag[:, 16 * r:16 * r + 16], T.x1[:]).then_inc(S.ld1, 16)
-    g.dma_start(T.x2s[:], T.x2[:]).then_inc(S.ld2, 16)
-    g.wait_ge(S.ld1, 16)
-    g.remote_dma_fused(
-        [RemoteDMATransfer(dst_ids=[did(T.cores[j]) for j in others], dma_engine_mask=0xFF, remote_sem=S.arr1,
-                           srcs=[T.ag[:, 16 * r:16 * r + 16]],
-                           dsts=[T.ag[:, 16 * r:16 * r + 16] for j in others])],
-        local_sem=S.sent)
-    g.wait_ge(S.ld2, 16)
-    g.dma_start(T.rs[:, r:r + 1], T.x2s[:, r:r + 1]).then_inc(S.own, 16)
-    for part in (others[:8], others[8:]):
+    if r is not None:
+        g.sync.dma_start(T.dg[r], T.x1[:]).then_inc(S.ldd, 16)
+        g.scalar.dma_start(T.x2s[:], T.x2[:]).then_inc(S.ldx, 16)
+        g.sync.dma_start(T.ag[:, 16 * r:16 * r + 16], T.x1[:]).then_inc(S.lda, 16)
+
+    for waits, transfers in prog[core]:
+        for w in waits:
+            g.wait_ge(S[w], total[w])
         g.remote_dma_fused(
-            [RemoteDMATransfer(dst_ids=[did(T.cores[j])], dma_engine_mask=1 << k, remote_sem=S.arr2,
-                               src=T.x2s[:, j:j + 1], dst=T.rs[:, r:r + 1])
-             for k, j in enumerate(part)],
+            [RemoteDMATransfer(dst_ids=[did(d) for d, _ in dsts], dma_engine_mask=mask, remote_sem=S[sem],
+                               srcs=[ap(s) for s in srcs], dsts=[ap(d) for _, d in dsts], alu_op=alu)
+             for srcs, dsts, mask, sem, alu in transfers],
             local_sem=S.sent)
-    g.wait_ge(S.arr1, 15 * 8)
-    g.dma_start(T.y1[:], T.ag[:]).then_inc(S.st1, 16)
-    g.wait_ge(S.own, 16)
-    g.wait_ge(S.arr2, 15)
-    n = 0
-    for w in (8, 4, 2, 1):
-        g.dma_start(T.rs[:, 0:w], T.rs[:, w:2 * w], accum_op=AluOpType.add).then_inc(S.acc, 16)
-        n += 16
-        g.wait_ge(S.acc, n)
-    g.dma_start(T.y2[:], T.rs[:, 0:1]).then_inc(S.st2, 16)
-    g.wait_ge(S.sent, 8 + 15)
-    g.wait_ge(S.st1, 16)
-    g.wait_ge(S.st2, 16)
+
+    if r is not None:
+        if core % 8 == 2:
+            j = 2 * ((core // 8 - 4) % 8) + 1
+            g.sync.wait_ge(S.in1, total["in1"])
+            g.sync.dma_start(T.ag[:, 16 * j:16 * j + 16], T.dg[j]).then_inc(S.cp, 16)
+            g.sync.wait_ge(S.cp, 16)
+        else:
+            g.sync.wait_ge(S.in2, total["in2"])
+        g.sync.wait_ge(S.lda, 16)
+        g.sync.wait_ge(S.fin, total["fin"])
+        g.sync.dma_start(T.y1[:], T.ag[:]).then_inc(S.st1, 16)
+        k = core % 8 - 2
+        g.scalar.wait_ge(S.ry, total["ry"])
+        g.scalar.dma_start(T.y2[:], T.y2l[:, k:k + 1]).then_inc(S.st2, 16)
+        g.sync.wait_ge(S.st1, 16)
+        g.scalar.wait_ge(S.st2, 16)
+    if total.get("sent"):
+        g.wait_ge(S.sent, total["sent"])

from concourse.bass import DstId, RemoteDMATransfer

SCRATCH = {
    "dg": ("dram", [16, 128, 16], "float32"),
    "ag": ("sbuf", [128, 256], "float32"),
    "x2s": ("sbuf", [128, 16], "bfloat16"),
    "xab": ("sbuf", [128, 32], "bfloat16"),
    "part": ("sbuf", [128, 16], "bfloat16"),
    "y2l": ("sbuf", [128, 2], "bfloat16"),
}
SEMAPHORES = ["ldd", "lda", "ldx", "cp", "st1", "st2",
              "in1", "in2", "fin",
              "rx", "rp", "ry",
              "sent"]


def _bits(mask):
    return bin(mask).count("1")


def _plan():
    prog = {k: [] for k in range(64)}

    def slot(j):
        return ("dg", j)

    def blk(j, n=1):
        return ("ag", 16 * j, 16 * (j + n))

    for c in range(8):
        m = c ^ 1

        def co(k, ch=c):
            return 8 * (ch % 8) + k

        def both(j):
            return [(co(2), blk(j)), (co(3), blk(j))]

        a, b = 2 * c, 2 * c + 1
        far_b = 2 * ((c - 4) % 8) + 1
        prog[co(2)] += [
            (["ldd"], [([slot(a)], [(co(4), slot(a)), (co(6, c + 2), slot(a)), (co(7, c + 4), slot(a)),
                                    (co(5, m), slot(a))], 0x00FF, "in1", 0),
                       ([slot(a)], [(co(3), blk(a))], 0xFF00, "fin", 0)]),
            (["ldx"], [([("x2s", 0, 16)], [(co(7), ("xab", 0, 16)), (co(1), ("xab", 0, 16))], 0xFFFF, "rx", 0)]),
            (["in1"], [([slot(far_b)], [(co(4, m), slot(far_b))], 0x00FF, "in2", 0),
                       ([slot(far_b)], [(co(3), blk(far_b))], 0xFF00, "fin", 0)]),
        ]
        relayed = 2 * ((m - 2) % 8)
        prog[co(3)] += [
            (["ldd"], [([slot(b)], [(co(4), slot(b)), (co(6, c + 2), slot(b)), (co(2, c + 4), slot(b)),
                                    (co(5, m), slot(b))], 0x00FF, "in1", 0),
                       ([slot(b)], [(co(2), blk(b))], 0xFF00, "fin", 0)]),
            (["ldx"], [([("x2s", 0, 16)], [(co(7), ("xab", 16, 32)), (co(1), ("xab", 16, 32))], 0xFFFF, "rx", 0)]),
            (["in2"], [([blk(relayed, 2)], [(co(2), blk(relayed, 2))], 0xFFFF, "fin", 0)]),
        ]
        x, y = 2 * ((m - 4) % 8) + 1, 2 * ((m + 2) % 8) + 1
        prog[co(4)] += [
            (["in1"], [([slot(a)], [(co(0, c - 2), slot(a))], 0x000F, "in2", 0),
                       ([slot(b)], [(co(0, c - 2), slot(b))], 0x00F0, "in2", 0)]),
            (["in2"], [([slot(x)], both(x), 0x00FF, "fin", 0), ([slot(y)], both(y), 0xFF00, "fin", 0)]),
        ]
        x, y = 2 * m, 2 * m + 1
        prog[co(5)] += [
            (["in1"], [([slot(x)], [(co(0, c - 2), slot(x))], 0x000F, "in2", 0),
                       ([slot(y)], [(co(4, c - 2), slot(y))], 0x00F0, "in2", 0),
                       ([slot(x)], both(x), 0x0F00, "fin", 0), ([slot(y)], both(y), 0xF000, "fin", 0)]),
        ]
        x, y = 2 * ((c - 2) % 8), 2 * ((c - 2) % 8) + 1
        prog[co(6)] += [
            (["in1"], [([slot(x)], [(co(3, m), blk(x))], 0x000F, "in2", 0),
                       ([slot(y)], [(co(3, m), blk(y))], 0x00F0, "in2", 0),
                       ([slot(x)], both(x), 0x0F00, "fin", 0), ([slot(y)], both(y), 0xF000, "fin", 0)]),
        ]
        x, y = 2 * ((c - 4) % 8), 2 * ((m - 4) % 8)
        cross = [d for d in range(8) if (d & 1) != (c & 1)]
        prog[co(7)] += [
            (["rx"], [([("xab", 2 * d, 2 * d + 2), ("xab", 16 + 2 * d, 16 + 2 * d + 2)],
                       [(co(1, d), ("part", 2 * c, 2 * c + 2))], 0x3 << (2 * i), "rp", 1)
                      for i, d in enumerate(cross)]),
            (["in1"], [([slot(x)], [(co(7, m), slot(x))], 0x00FF, "in2", 0), ([slot(x)], both(x), 0xFF00, "fin", 0)]),
            (["in2"], [([slot(y)], both(y), 0xFFFF, "fin", 0)]),
        ]
        x, y, z = 2 * ((c + 2) % 8), 2 * ((c + 2) % 8) + 1, 2 * ((m + 2) % 8)
        prog[co(0)] += [
            (["in2"], [([slot(x)], both(x), 0x000F, "fin", 0), ([slot(y)], both(y), 0x00F0, "fin", 0),
                       ([slot(z)], both(z), 0x0F00, "fin", 0)]),
        ]
        plane = [d for d in range(8) if (d & 1) == (c & 1) and d != c]
        prog[co(1)] += [
            (["rx"], [([("xab", 2 * d, 2 * d + 2), ("xab", 16 + 2 * d, 16 + 2 * d + 2)],
                       [(co(1, d), ("part", 2 * c, 2 * c + 2))], 0x3 << (2 * i), "rp", 1)
                      for i, d in enumerate(plane)]),
            (["rp"], [([("part", 2 * d, 2 * d + 2) for d in range(8) if d != c]
                       + [("xab", 2 * c, 2 * c + 2), ("xab", 16 + 2 * c, 16 + 2 * c + 2)],
                       [(co(2), ("y2l", 0, 2)), (co(3), ("y2l", 0, 2))], 0xFFFF, "ry", 1)]),
        ]
    return prog


def _totals(prog):
    total = {k: {} for k in range(64)}
    for core, calls in prog.items():
        for _waits, transfers in calls:
            for _srcs, dsts, mask, sem, _alu in transfers:
                total[core]["sent"] = total[core].get("sent", 0) + _bits(mask)
                for dst, _ap in dsts:
                    total[dst][sem] = total[dst].get(sem, 0) + _bits(mask)
    return total


def rank_program(g, core, T, topo):
    prog = _plan()
    total = _totals(prog)[core]
    for name in ("ldd", "lda", "ldx", "cp", "st1", "st2"):
        total[name] = 16
    S = T.sem
    r = T.rank_of(core)

    def ap(d):
        if d[0] == "dg":
            return T.dg[d[1]]
        return T[d[0]][:, d[1]:d[2]]

    def did(c):
        rid, pid, _se = topo.addr(c)
        return DstId(rid=rid, pnc=pid)

    if r is not None:
        g.sync.dma_start(T.dg[r], T.x1[:]).then_inc(S.ldd, 16)
        g.scalar.dma_start(T.x2s[:], T.x2[:]).then_inc(S.ldx, 16)
        g.sync.dma_start(T.ag[:, 16 * r:16 * r + 16], T.x1[:]).then_inc(S.lda, 16)

    for waits, transfers in prog[core]:
        for w in waits:
            g.wait_ge(S[w], total[w])
        g.remote_dma_fused(
            [RemoteDMATransfer(dst_ids=[did(d) for d, _ in dsts], dma_engine_mask=mask, remote_sem=S[sem],
                               srcs=[ap(s) for s in srcs], dsts=[ap(d) for _, d in dsts], alu_op=alu)
             for srcs, dsts, mask, sem, alu in transfers],
            local_sem=S.sent)

    if r is not None:
        if core % 8 == 2:
            j = 2 * ((core // 8 - 4) % 8) + 1
            g.sync.wait_ge(S.in1, total["in1"])
            g.sync.dma_start(T.ag[:, 16 * j:16 * j + 16], T.dg[j]).then_inc(S.cp, 16)
            g.sync.wait_ge(S.cp, 16)
        else:
            g.sync.wait_ge(S.in2, total["in2"])
        g.sync.wait_ge(S.lda, 16)
        g.sync.wait_ge(S.fin, total["fin"])
        g.sync.dma_start(T.y1[:], T.ag[:]).then_inc(S.st1, 16)
        k = core % 8 - 2
        g.scalar.wait_ge(S.ry, total["ry"])
        g.scalar.dma_start(T.y2[:], T.y2l[:, k:k + 1]).then_inc(S.st2, 16)
        g.sync.wait_ge(S.st1, 16)
        g.scalar.wait_ge(S.st2, 16)
    if total.get("sent"):
        g.wait_ge(S.sent, total["sent"])
